import numpy as np
import ml_dtypes


def mxq(x, axis, fmt="e4m3"):
    dtype, down = {"e4m3": (ml_dtypes.float8_e4m3fn, 7), "e5m2": (ml_dtypes.float8_e5m2, 14)}[fmt]
    v = np.moveaxis(np.asarray(x, np.float32).astype(ml_dtypes.bfloat16).astype(np.float64), axis, -1)
    blocks = v.reshape(v.shape[:-1] + (-1, 32))
    amax = np.abs(blocks).max(-1, keepdims=True)
    byte = np.maximum(np.where(amax > 0, np.frexp(amax)[1] - 1 + 127, 0) - down, 1)
    scale = np.exp2(byte - 127.0)
    codes = (blocks / scale).astype(np.float32).astype(dtype).astype(np.float64)
    return np.moveaxis((codes * scale).reshape(v.shape), -1, axis)


WIDE = False


def mx_kscale(k):
    if not WIDE:
        return np.ones(k)
    levels = np.array([30, -30])
    if k % 512:
        return np.exp2(np.random.permutation(np.resize(levels, k // 32))).repeat(32)
    a = np.empty((k // 512, 16))
    for p in range(k // 512):
        a[p, :8] = np.random.permutation(np.resize(levels, 8))
        for g in range(8):
            far = levels[np.abs(levels - a[p, g]) >= 10]
            a[p, g + 8] = far[np.random.randint(len(far))]
    return np.exp2(a.ravel()).repeat(32)


BF16 = ml_dtypes.bfloat16


def bf(x):
    return np.asarray(x, np.float32).astype(BF16)


def f64(x):
    return np.asarray(x).astype(np.float64)


E2M1 = np.array([0.0, 0.5, 1.0, 1.5, 2.0, 3.0, 4.0, 6.0, -0.0, -0.5, -1.0, -1.5, -2.0, -3.0, -4.0, -6.0])


def pack_weight(w, fmt):
    k, n = w.shape
    w = f64(bf(w)).reshape(k // 32, 32, n)
    amax = np.abs(w).max(1)
    if fmt == "e4m3":
        byte = np.frexp(amax)[1] - 1 + 127 - 7
    else:
        mant, ex = np.frexp(amax / 6.0)
        byte = np.where(mant > 0.5, ex, ex - 1) + 127
    byte = np.clip(np.where(amax > 0, byte, 1), 1, 254)
    scaled = (w * np.exp2(127.0 - byte)[:, None, :]).reshape(k, n).astype(np.float32)
    by_word = np.ascontiguousarray(scaled.reshape(k // 512, 128, 4, n).transpose(0, 1, 3, 2))
    if fmt == "e4m3":
        words = by_word.astype(ml_dtypes.float8_e4m3fn).view(np.uint8)
    else:
        c = by_word.astype(ml_dtypes.float4_e2m1fn).view(np.uint8) & 0xF
        words = c[..., 0::2] | (c[..., 1::2] << 4)
    return np.ascontiguousarray(words), np.ascontiguousarray(byte.astype(np.uint8).reshape(k // 512, 16, n))


def unpack_weight(words, scales, fmt):
    g, p, n, _ = words.shape
    if fmt == "e4m3":
        vals = np.ascontiguousarray(words).view(ml_dtypes.float8_e4m3fn).astype(np.float64)
    else:
        nib = np.empty((g, p, n, 4), np.uint8)
        nib[..., 0::2] = words & 0xF
        nib[..., 1::2] = words >> 4
        vals = E2M1[nib]
    vals = vals * np.repeat(np.exp2(scales.astype(np.float64) - 127.0), 8, axis=1)[..., None]
    return vals.transpose(0, 1, 3, 2).reshape(g * 512, n)
def pack4(w):
    words, scales = pack_weight(w, "e2m1")
    return words.reshape(words.shape[0], 128, -1), scales


def unpack4(words, scales):
    return unpack_weight(words.reshape(words.shape[0], 128, -1, 2), scales, "e2m1")


P, C, N = 4096, 512, 1024


def setup_inputs():
    s = mx_kscale(P)
    u = mx_kscale(C)
    a = np.random.standard_normal((P, C)) * s[:, None] * u
    b = np.random.standard_normal((P, N)) / np.sqrt(P) / s[:, None]
    target = np.random.standard_normal((C, N)) * u[:, None]
    weight = (0.5 + np.random.random_sample(C)) / np.sqrt(C) / u ** 2
    guide = (0.5 + np.random.random_sample(P)) / s
    b_words, b_scales = pack4(b)
    return {"a": bf(a),
            "b_words": b_words,
            "b_scales": b_scales,
            "target": bf(target),
            "weight": bf(weight),
            "guide": bf(guide)}


def reference(a, b_words, b_scales, target, weight, guide):
    a = f64(a)
    b = unpack4(b_words, b_scales)
    gram = mxq(a, 0, "e4m3").T @ b
    diff = f64(weight)[:, None] * (gram - f64(target))
    grad = mxq(a, 1, "e4m3") @ mxq(diff, 0, "e5m2")
    return f64(guide)[:, None] * grad

@@ -1,0 +1,326 @@
+from contextlib import ExitStack
+
+import concourse.mybir as mybir
+from concourse.masks import make_identity
+
+POS, CH, OUT = 4096, 512, 1024
+FLOPS = 2 * 2 * POS * CH * OUT
+
+F32 = mybir.dt.float32
+BF16 = mybir.dt.bfloat16
+I32 = mybir.dt.int32
+U32 = mybir.dt.uint32
+U8 = mybir.dt.uint8
+E4M3 = mybir.dt.float8_e4m3fn_x4
+E5M2 = mybir.dt.float8_e5m2_x4
+E2M1 = mybir.dt.float4_e2m1fn_x4
+ALU = mybir.AluOpType
+ACT = mybir.ActivationFunctionType
+
+P = 128
+PACK = 4
+GROUP = P * PACK
+GROUPS = POS // GROUP
+HALF = 512
+SPLIT = [60,60,60,60,60,52,60,60]
+FILL = [7,2,3,0,15]
+PER = [1]
+ER = [0,1,3,5]
+VT = [2]
+TR3 = 11
+QE1 = 6
+SN1 = 0
+EARLY = 3
+SCALAR_N = 176
+
+
+def tile_cross_gram_texture_gradient_s9_kernel(tc, a, b_words, b_scales, target, weight, guide, out):
+    nc = tc.nc
+    with ExitStack() as ctx:
+        keep = ctx.enter_context(tc.tile_pool(name="keep", bufs=1))
+        stage = ctx.enter_context(tc.tile_pool(name="stage", bufs=3))
+        outs = ctx.enter_context(tc.tile_pool(name="outs", bufs=8))
+        psum = ctx.enter_context(tc.psum_pool(name="psum", bufs=1))
+        ctx.enter_context(tc.manual_schedule())
+
+        def bank(i):
+            return psum.tile([P, HALF], F32, name="bank%d" % i)
+
+        raw, b_code, b_scale, tgt, wtgt = {}, {}, {}, {}, {}
+        a_pos, a_pos_q, turned, a_ch, a_ch_q = {}, {}, {}, {}, {}
+        gram, err, err_q, result, closed = {}, {}, {}, {}, {}
+
+        ident = keep.tile([P, P], F32, name="ident")
+        rows = keep.tile([P, GROUP], BF16, name="rows")
+        cols = keep.tile([P, GROUPS + 1, PACK], F32, name="cols")
+
+        def load_a(g):
+            raw[g] = keep.tile([P, PACK, CH], BF16, name="raw%d" % g, align_bytes=64)
+            nc.sync.dma_start(out=raw[g][:], in_=a[g * GROUP:(g + 1) * GROUP, :].rearrange("(p j) c -> p j c", j=PACK))
+
+        def load_b(h, g0, n):
+            t = keep.tile([P, n, 2 * HALF], U8, name="bw%d_%d" % (h, g0), align_bytes=64)
+            src = b_words[g0:g0 + n, :, 2 * HALF * h:2 * HALF * (h + 1)].rearrange("g p n -> p g n")
+            nc.sync.dma_start(out=t[:].bitcast(I32), in_=src.bitcast(I32))
+            for i in range(n):
+                b_code[h, g0 + i] = t[:, i, :]
+
+        def clear_scales(h, engine):
+            b_scale[h] = keep.tile([P, GROUPS, HALF], U8, name="bs%d" % h, align_bytes=64)
+            engine.memset(b_scale[h][:].bitcast(I32), 0)
+
+        def load_scales(h):
+            for q in range(4):
+                src = b_scales[:, 4 * q:4 * q + 4, HALF * h:HALF * (h + 1)].rearrange("g r n -> r g n")
+                nc.sync.dma_start(out=b_scale[h][32 * q:32 * q + 4, :, :].bitcast(I32), in_=src.bitcast(I32))
+
+        def load_target(h):
+            tgt[h] = keep.tile([P, PACK, HALF], BF16, name="tgt%d" % h)
+            nc.sync.dma_start(out=tgt[h][:], in_=target[:, HALF * h:HALF * (h + 1)].rearrange("(p t) n -> p t n", t=PACK))
+
+        def turn_vectors(bk):
+            pt = bank(bk)
+            words = rows[:].bitcast(F32)
+            for u in range(2):
+                nc.tensor.transpose(out=pt[:, u * P:(u + 1) * P], in_=words[:, u:2 * P:2], identity=ident[:])
+            turned["vectors"] = pt
+
+        def copy_vectors():
+            pt = turned["vectors"]
+            view = pt[:, 0:2 * P].bitcast(BF16).rearrange("p (u r e) -> p r u e", u=2, e=2)
+            nc.vector.tensor_copy(out=cols[:].rearrange("p r (u e) -> p r u e", u=2), in_=view[:, 0:GROUPS + 1, :, :])
+
+        def interleave_a(g, split):
+            a_pos[g] = stage.tile([P, PACK, P, PACK], BF16, name="a_pos", align_bytes=64)
+            dst = a_pos[g][:].rearrange("p t m j -> p m t j")
+            src = raw[g][:].rearrange("p j (m t) -> p m t j", t=PACK)
+            nc.vector.tensor_copy(out=dst[:, split:P], in_=src[:, split:P])
+            nc.scalar.copy(out=dst[:, 0:split], in_=src[:, 0:split])
+
+        def quantize(name, src, fmt):
+            width = src.shape[1] // PACK
+            codes = keep.tile([P, width], U32, name="c_" + name, align_bytes=64)
+            scales = keep.tile([P, width], U8, name="s_" + name, align_bytes=64)
+            nc.vector.quantize_mx(out=codes[:].bitcast(fmt), scales=scales[:], in_=src)
+            return codes, scales
+
+        def quantize_a_pos(g):
+            a_pos_q[g] = quantize("ap%d" % g, a_pos[g][:].rearrange("p t m j -> p (t m j)"), E4M3)
+
+        def gram_pass(h, t, g, bk):
+            if g == 0:
+                gram[h, t] = bank(bk)
+            closed[h, t] = g == GROUPS - 1
+            codes, scales = a_pos_q[g]
+            nc.tensor.matmul_mx(
+                out=gram[h, t][:], lhsT=codes[:, t * P:(t + 1) * P].bitcast(E4M3), lhsT_scale=scales[:, t * P:(t + 1) * P],
+                rhs=b_code[h, g].bitcast(E2M1), rhs_scale=b_scale[h][:, g, :], start=(g == 0), stop=(g == GROUPS - 1))
+
+        def turn_a(g, banks):
+            words = raw[g][:].rearrange("p j c -> p (j c)").bitcast(F32)
+            for s in range(2):
+                turned[g, s] = bank(banks[s])
+                for jj in range(2):
+                    for u in range(2):
+                        w0 = (2 * s + jj) * 2 * P + u
+                        c0 = (2 * jj + u) * P
+                        nc.tensor.transpose(out=turned[g, s][:, c0:c0 + P], in_=words[:, w0:w0 + 2 * P - u:2], identity=ident[:])
+
+        def copy_turned(g, s, on_vector):
+            if s == 0:
+                a_ch[g] = stage.tile([P, 2, 2 * P * 2], F32, name="a_ch", align_bytes=64)
+            dst = a_ch[g][:, s, :].rearrange("p (j r u) -> p j r u", j=2, u=2)
+            src = turned[g, s][:].rearrange("p (j u r) -> p j r u", j=2, u=2)
+            if on_vector:
+                nc.vector.tensor_copy(out=dst, in_=src)
+            else:
+                nc.scalar.copy(out=dst, in_=src)
+
+        def quantize_a_ch(g):
+            a_ch_q[g] = quantize("ac%d" % g, a_ch[g][:].rearrange("p s w -> p (s w)").bitcast(BF16), E4M3)
+
+        def weigh_target(h, t, on_vector):
+            if t == 0:
+                wtgt[h] = keep.tile([P, PACK, HALF], F32, name="wtgt%d" % h)
+            if on_vector == 2:
+                nc.gpsimd.tensor_scalar(out=wtgt[h][:, t, :], in0=tgt[h][:, t, :], scalar1=cols[:, GROUPS, t:t + 1],
+                                        scalar2=0.0, op0=ALU.mult, op1=ALU.add)
+            elif on_vector:
+                nc.vector.tensor_scalar_mul(out=wtgt[h][:, t, :], in0=tgt[h][:, t, :], scalar1=cols[:, GROUPS, t:t + 1])
+            else:
+                nc.scalar.activation(out=wtgt[h][:, t, :], in_=tgt[h][:, t, :], func=ACT.Copy, scale=cols[:, GROUPS, t:t + 1])
+
+        def error(h, t):
+            assert closed[h, t]
+            if t == 0:
+                err[h] = keep.tile([P, PACK, HALF], BF16, name="err%d" % h)
+            nc.vector.scalar_tensor_tensor(
+                out=err[h][:, t, :], in0=gram[h, t][:], scalar=cols[:, GROUPS, t:t + 1], in1=wtgt[h][:, t, :],
+                op0=ALU.mult, op1=ALU.subtract)
+
+        def quantize_error(h, scalar_n):
+            grouped = keep.tile([P, HALF, PACK], BF16, name="eg%d" % h, align_bytes=64)
+            dst = grouped[:].rearrange("p (c i) t -> p c t i", i=4)
+            src = err[h][:].rearrange("p t (c i) -> p c t i", i=4)
+            split = scalar_n // 4
+            nc.vector.tensor_copy(out=dst[:, split:], in_=src[:, split:])
+            if split:
+                nc.scalar.copy(out=dst[:, 0:split], in_=src[:, 0:split])
+            err_q[h] = quantize("e%d" % h, grouped[:].rearrange("p n t -> p (n t)"), E5M2)
+
+        def out_tile(g, j, h, bk, dst, on_vector):
+            acc = bank(bk)
+            codes, scales = a_ch_q[g]
+            e_codes, e_scales = err_q[h]
+            nc.tensor.matmul_mx(
+                out=acc[:], lhsT=codes[:, j * P:(j + 1) * P].bitcast(E4M3), lhsT_scale=scales[:, j * P:(j + 1) * P],
+                rhs=e_codes[:].bitcast(E5M2), rhs_scale=e_scales[:], start=True, stop=True)
+            if on_vector:
+                nc.vector.tensor_scalar_mul(out=dst, in0=acc[:], scalar1=cols[:, g, j:j + 1])
+            else:
+                nc.scalar.activation(out=dst, in_=acc[:], func=ACT.Copy, scale=cols[:, g, j:j + 1])
+
+        def out_rows(g):
+            return out[g * GROUP:(g + 1) * GROUP, :].rearrange("(p j) n -> p j n", j=PACK)
+
+        def half_tile(g, j, h, bk, on_vector, per_store):
+            if j == 0:
+                result[g, h] = outs.tile([P, PACK, HALF], F32, name="result")
+            out_tile(g, j, h, bk, result[g, h][:, j, :], on_vector)
+            if (j + 1) % per_store == 0:
+                js = slice(j + 1 - per_store, j + 1)
+                nc.sync.dma_start(out=out_rows(g)[:, js, HALF * h:HALF * (h + 1)], in_=result[g, h][:, js, :])
+
+        def full_tile(g, j, h, bk, on_vector, per_store):
+            if j % 2 == 0 and h == 0:
+                result[g, j // 2] = outs.tile([P, 2, OUT], F32, name="result")
+            out_tile(g, j, h, bk, result[g, j // 2][:, j % 2, HALF * h:HALF * (h + 1)], on_vector)
+            if (j + 1) % per_store == 0 and h == 1:
+                j0 = j + 1 - per_store
+                nc.sync.dma_start(out=out_rows(g)[:, j0:j + 1, :], in_=result[g, j // 2][:, j0 % 2:j % 2 + 1, :])
+
+        nc.vector.memset(rows[:].bitcast(I32), 0)
+        clear_scales(0, nc.vector)
+        make_identity(nc, ident[:])
+        clear_scales(1, nc.gpsimd)
+        load_a(0)
+        nc.scalar.dma_start(out=rows[0:GROUPS, :], in_=guide.rearrange("(g c) -> g c", g=GROUPS))
+        nc.scalar.dma_start(out=rows[GROUPS:GROUPS + 1, :], in_=weight.rearrange("(g c) -> g c", g=1))
+        load_a(1)
+        load_scales(0)
+        load_b(0, 0, 2)
+        load_a(2)
+        load_a(3)
+        load_b(0, 2, 2)
+        load_scales(1)
+        load_b(1, 0, 4)
+        load_a(4)
+        load_a(5)
+        load_b(0, 4, 2)
+        load_a(6)
+        load_a(7)
+        load_b(0, 6, 2)
+        load_target(0)
+        load_target(1)
+        load_b(1, 4, 4)
+
+        turn_vectors(3)
+        turn_a(0, (4, 5))
+        turn_a(1, (6, 7))
+        fill = [(t, g) for g in range(4) for t in (2, 3, 0, 1)] + [(t, g) for t in range(PACK) for g in range(4, GROUPS)]
+        nxt = 0
+
+        def second(i):
+            t, g = fill[i]
+            gram_pass(1, t, g, 4 + t)
+
+        def first(g):
+            for t in range(PACK):
+                gram_pass(0, t, g, t)
+
+        def seconds(start, count):
+            for i in range(start, min(start + count, len(fill))):
+                second(i)
+            return min(start + count, len(fill))
+
+        interleave_a(0, SPLIT[0])
+        copy_vectors()
+        interleave_a(1, SPLIT[1])
+        quantize_a_pos(0)
+        quantize_a_pos(1)
+        for g in range(2):
+            copy_turned(g, 0, True)
+            copy_turned(g, 1, False)
+        first(0)
+        first(1)
+        interleave_a(2, SPLIT[2])
+        quantize_a_ch(0)
+        quantize_a_pos(2)
+        first(2)
+        turn_a(2, (4, 5))
+        interleave_a(3, SPLIT[3])
+        quantize_a_pos(3)
+        first(3)
+        quantize_a_ch(1)
+        copy_turned(2, 0, False)
+        copy_turned(2, 1, False)
+        nxt = seconds(nxt, FILL[0])
+        interleave_a(4, SPLIT[4])
+        quantize_a_ch(2)
+        quantize_a_pos(4)
+        first(4)
+        interleave_a(5, SPLIT[5])
+        quantize_a_pos(5)
+        nxt = seconds(nxt, FILL[1])
+        first(5)
+        interleave_a(6, SPLIT[6])
+        interleave_a(7, SPLIT[7])
+        quantize_a_pos(6)
+        quantize_a_pos(7)
+        nxt = seconds(nxt, FILL[2])
+        first(6)
+        first(7)
+        for t in range(PACK):
+            weigh_target(0, t, False)
+            error(0, t)
+        weigh_target(1, 0, False)
+        weigh_target(1, 1, False)
+        quantize_error(0, SCALAR_N)
+        weigh_target(1, 2, False)
+        weigh_target(1, 3, False)
+        nxt = seconds(nxt, FILL[4])
+
+        for n in range(EARLY * PACK):
+            g, j = divmod(n, PACK)
+            half_tile(g, j, 0, n % 4, n in VT, 1 if n < 2 else 2)
+            nxt = seconds(nxt, PER[min(n, len(PER) - 1)])
+            for t in range(PACK):
+                if ER[t] == n:
+                    error(1, t)
+            if n == TR3:
+                turn_a(3, (4, 5) if TR3 < 11 else (6, 7))
+            if n == QE1:
+                quantize_error(1, SN1)
+        nxt_g = 3
+
+        n = 0
+        for k in range(EARLY):
+            for j in range(PACK):
+                half_tile(k, j, 1, n % 4, n % 2 == 1, 2)
+                n = n + 1
+                if k == 0 and j < 2:
+                    copy_turned(nxt_g, j, j == 0)
+                if k == 0 and j == 3:
+                    quantize_a_ch(nxt_g)
+        for g in range(EARLY, GROUPS):
+            ahead = g + 1 if g + 1 < GROUPS else None
+            if ahead:
+                turn_a(ahead, (6, 7))
+            for j in range(PACK):
+                for h in range(2):
+                    full_tile(g, j, h, n % 6, n % 2 == 1, 1 if g == GROUPS - 1 else 2)
+                    n = n + 1
+                if ahead and j < 2:
+                    copy_turned(ahead, j, j == 1)
+                if ahead and j == 2:
+                    quantize_a_ch(ahead)

@@ -22,15 +22,19 @@ PACK = 4
 GROUP = P * PACK
 GROUPS = POS // GROUP
 HALF = 512
-SPLIT = [60,60,60,60,60,52,60,60]
-FILL = [7,2,3,0,15]
-PER = [1]
-ER = [0,1,3,5]
-VT = [2]
-TR3 = 11
-QE1 = 6
-SN1 = 0
-EARLY = 3
+SPLIT = [44,44,60,60,60,44,44,60]
+FILL = [4,6,0,3,0,14]
+PAIR = False
+W1 = 0
+W1V = True
+PER = 1
+ER = [0,1,2,4]
+VT = []
+TR2 = 5
+QE1 = 4
+SN1 = 96
+EARLY = 2
+PS = 2
 SCALAR_N = 176
 
 
@@ -58,25 +62,29 @@ def tile_cross_gram_texture_gradient_s9_kernel(tc, a, b_words, b_scales, target,
             raw[g] = keep.tile([P, PACK, CH], BF16, name="raw%d" % g, align_bytes=64)
             nc.sync.dma_start(out=raw[g][:], in_=a[g * GROUP:(g + 1) * GROUP, :].rearrange("(p j) c -> p j c", j=PACK))
 
-        def load_b(h, g0, n):
-            t = keep.tile([P, n, 2 * HALF], U8, name="bw%d_%d" % (h, g0), align_bytes=64)
-            src = b_words[g0:g0 + n, :, 2 * HALF * h:2 * HALF * (h + 1)].rearrange("g p n -> p g n")
+        def load_b(g0, n, h0, halves):
+            t = keep.tile([P, n, halves * 2 * HALF], U8, name="bw%d_%d" % (g0, h0), align_bytes=64)
+            src = b_words[g0:g0 + n, :, 2 * HALF * h0:2 * HALF * (h0 + halves)].rearrange("g p n -> p g n")
             nc.sync.dma_start(out=t[:].bitcast(I32), in_=src.bitcast(I32))
             for i in range(n):
-                b_code[h, g0 + i] = t[:, i, :]
+                for h in range(halves):
+                    b_code[h0 + h, g0 + i] = t[:, i, 2 * HALF * h:2 * HALF * (h + 1)]
 
-        def clear_scales(h, engine):
-            b_scale[h] = keep.tile([P, GROUPS, HALF], U8, name="bs%d" % h, align_bytes=64)
-            engine.memset(b_scale[h][:].bitcast(I32), 0)
+        def clear_scales(s, engine):
+            b_scale[s] = keep.tile([P, 4, OUT], U8, name="bs%d" % s, align_bytes=64)
+            engine.memset(b_scale[s][:].bitcast(I32), 0)
 
-        def load_scales(h):
-            for q in range(4):
-                src = b_scales[:, 4 * q:4 * q + 4, HALF * h:HALF * (h + 1)].rearrange("g r n -> r g n")
-                nc.sync.dma_start(out=b_scale[h][32 * q:32 * q + 4, :, :].bitcast(I32), in_=src.bitcast(I32))
+        def load_scales(s):
+            for r in range(4):
+                src = b_scales[4 * s:4 * s + 4, r:16:4, :].rearrange("g q n -> q g n")
+                nc.sync.dma_start(out=b_scale[s][r:P:32, :, :].bitcast(I32), in_=src.bitcast(I32))
 
-        def load_target(h):
-            tgt[h] = keep.tile([P, PACK, HALF], BF16, name="tgt%d" % h)
-            nc.sync.dma_start(out=tgt[h][:], in_=target[:, HALF * h:HALF * (h + 1)].rearrange("(p t) n -> p t n", t=PACK))
+        def load_target(h, t0, n):
+            tile = keep.tile([P, n, HALF], BF16, name="tgt%d_%d" % (h, t0))
+            src = target[:, HALF * h:HALF * (h + 1)].rearrange("(p t) n -> p t n", t=PACK)
+            nc.sync.dma_start(out=tile[:], in_=src[:, t0:t0 + n, :])
+            for i in range(n):
+                tgt[h, t0 + i] = tile[:, i, :]
 
         def turn_vectors(bk):
             pt = bank(bk)
@@ -92,10 +100,10 @@ def tile_cross_gram_texture_gradient_s9_kernel(tc, a, b_words, b_scales, target,
 
         def interleave_a(g, split):
             a_pos[g] = stage.tile([P, PACK, P, PACK], BF16, name="a_pos", align_bytes=64)
-            dst = a_pos[g][:].rearrange("p t m j -> p m t j")
-            src = raw[g][:].rearrange("p j (m t) -> p m t j", t=PACK)
-            nc.vector.tensor_copy(out=dst[:, split:P], in_=src[:, split:P])
-            nc.scalar.copy(out=dst[:, 0:split], in_=src[:, 0:split])
+            dst = a_pos[g][:].rearrange("p t (b m) j -> p b t m j", m=2)
+            src = raw[g][:].rearrange("p j (b m t) -> p b t m j", m=2, t=PACK)
+            nc.vector.tensor_copy(out=dst[:, split // 2:], in_=src[:, split // 2:])
+            nc.scalar.copy(out=dst[:, 0:split // 2], in_=src[:, 0:split // 2])
 
         def quantize(name, src, fmt):
             width = src.shape[1] // PACK
@@ -107,6 +115,16 @@ def tile_cross_gram_texture_gradient_s9_kernel(tc, a, b_words, b_scales, target,
         def quantize_a_pos(g):
             a_pos_q[g] = quantize("ap%d" % g, a_pos[g][:].rearrange("p t m j -> p (t m j)"), E4M3)
 
+        def quantize_a_pos_by_slot(g):
+            codes = keep.tile([P, GROUP], U32, name="c_ap%d" % g, align_bytes=64)
+            scales = keep.tile([P, GROUP], U8, name="s_ap%d" % g, align_bytes=64)
+            a_pos_q[g] = codes, scales
+            for t in range(PACK):
+                nc.vector.quantize_mx(
+                    out=codes[:, t * P:(t + 1) * P].bitcast(E4M3), scales=scales[:, t * P:(t + 1) * P],
+                    in_=a_pos[g][:, t, :, :].rearrange("p m j -> p (m j)"))
+                gram_pass(0, t, g, t)
+
         def gram_pass(h, t, g, bk):
             if g == 0:
                 gram[h, t] = bank(bk)
@@ -114,7 +132,7 @@ def tile_cross_gram_texture_gradient_s9_kernel(tc, a, b_words, b_scales, target,
             codes, scales = a_pos_q[g]
             nc.tensor.matmul_mx(
                 out=gram[h, t][:], lhsT=codes[:, t * P:(t + 1) * P].bitcast(E4M3), lhsT_scale=scales[:, t * P:(t + 1) * P],
-                rhs=b_code[h, g].bitcast(E2M1), rhs_scale=b_scale[h][:, g, :], start=(g == 0), stop=(g == GROUPS - 1))
+                rhs=b_code[h, g].bitcast(E2M1), rhs_scale=b_scale[g // 4][:, g % 4, HALF * h:HALF * (h + 1)], start=(g == 0), stop=(g == GROUPS - 1))
 
         def turn_a(g, banks):
             words = raw[g][:].rearrange("p j c -> p (j c)").bitcast(F32)
@@ -143,15 +161,16 @@ def tile_cross_gram_texture_gradient_s9_kernel(tc, a, b_words, b_scales, target,
             if t == 0:
                 wtgt[h] = keep.tile([P, PACK, HALF], F32, name="wtgt%d" % h)
             if on_vector == 2:
-                nc.gpsimd.tensor_scalar(out=wtgt[h][:, t, :], in0=tgt[h][:, t, :], scalar1=cols[:, GROUPS, t:t + 1],
+                nc.gpsimd.tensor_scalar(out=wtgt[h][:, t, :], in0=tgt[h, t], scalar1=cols[:, GROUPS, t:t + 1],
                                         scalar2=0.0, op0=ALU.mult, op1=ALU.add)
             elif on_vector:
-                nc.vector.tensor_scalar_mul(out=wtgt[h][:, t, :], in0=tgt[h][:, t, :], scalar1=cols[:, GROUPS, t:t + 1])
+                nc.vector.tensor_scalar_mul(out=wtgt[h][:, t, :], in0=tgt[h, t], scalar1=cols[:, GROUPS, t:t + 1])
             else:
-                nc.scalar.activation(out=wtgt[h][:, t, :], in_=tgt[h][:, t, :], func=ACT.Copy, scale=cols[:, GROUPS, t:t + 1])
+                nc.scalar.activation(out=wtgt[h][:, t, :], in_=tgt[h, t], func=ACT.Copy, scale=cols[:, GROUPS, t:t + 1])
 
         def error(h, t):
             assert closed[h, t]
+            closed["e", h, t] = True
             if t == 0:
                 err[h] = keep.tile([P, PACK, HALF], BF16, name="err%d" % h)
             nc.vector.scalar_tensor_tensor(
@@ -159,6 +178,7 @@ def tile_cross_gram_texture_gradient_s9_kernel(tc, a, b_words, b_scales, target,
                 op0=ALU.mult, op1=ALU.subtract)
 
         def quantize_error(h, scalar_n):
+            assert all(closed["e", h, t] for t in range(PACK))
             grouped = keep.tile([P, HALF, PACK], BF16, name="eg%d" % h, align_bytes=64)
             dst = grouped[:].rearrange("p (c i) t -> p c t i", i=4)
             src = err[h][:].rearrange("p t (c i) -> p c t i", i=4)
@@ -206,121 +226,115 @@ def tile_cross_gram_texture_gradient_s9_kernel(tc, a, b_words, b_scales, target,
         load_a(0)
         nc.scalar.dma_start(out=rows[0:GROUPS, :], in_=guide.rearrange("(g c) -> g c", g=GROUPS))
         nc.scalar.dma_start(out=rows[GROUPS:GROUPS + 1, :], in_=weight.rearrange("(g c) -> g c", g=1))
-        load_a(1)
         load_scales(0)
-        load_b(0, 0, 2)
+        load_b(0, 1, 0, 2)
+        load_a(1)
+        load_b(1, 1, 0, 2)
         load_a(2)
         load_a(3)
-        load_b(0, 2, 2)
-        load_scales(1)
-        load_b(1, 0, 4)
+        load_b(2, 2, 0, 2)
         load_a(4)
+        load_scales(1)
         load_a(5)
-        load_b(0, 4, 2)
+        load_b(4, 2, 0, 1)
         load_a(6)
         load_a(7)
-        load_b(0, 6, 2)
-        load_target(0)
-        load_target(1)
-        load_b(1, 4, 4)
+        load_b(6, 2, 0, 1)
+        load_target(0, 0, 2)
+        load_target(0, 2, 2)
+        load_b(4, 4, 1, 1)
+        load_target(1, 0, 4)
 
-        turn_vectors(3)
-        turn_a(0, (4, 5))
-        turn_a(1, (6, 7))
-        fill = [(t, g) for g in range(4) for t in (2, 3, 0, 1)] + [(t, g) for t in range(PACK) for g in range(4, GROUPS)]
-        nxt = 0
-
-        def second(i):
-            t, g = fill[i]
-            gram_pass(1, t, g, 4 + t)
+        fill = [(t, g) for g in range(4) for t in range(PACK)] + [(t, g) for t in range(PACK) for g in range(4, GROUPS)]
 
         def first(g):
             for t in range(PACK):
                 gram_pass(0, t, g, t)
 
         def seconds(start, count):
-            for i in range(start, min(start + count, len(fill))):
-                second(i)
-            return min(start + count, len(fill))
+            stop = min(start + count, len(fill))
+            for t, g in fill[start:stop]:
+                gram_pass(1, t, g, 4 + t)
+            return stop
 
+        turn_vectors(3)
+        turn_a(0, (4, 5))
         interleave_a(0, SPLIT[0])
         copy_vectors()
-        interleave_a(1, SPLIT[1])
         quantize_a_pos(0)
-        quantize_a_pos(1)
-        for g in range(2):
-            copy_turned(g, 0, True)
-            copy_turned(g, 1, False)
+        copy_turned(0, 0, True)
+        copy_turned(0, 1, False)
         first(0)
+        turn_a(1, (6, 7))
+        interleave_a(1, SPLIT[1])
+        quantize_a_ch(0)
+        quantize_a_pos(1)
         first(1)
         interleave_a(2, SPLIT[2])
-        quantize_a_ch(0)
+        copy_turned(1, 0, True)
+        copy_turned(1, 1, False)
         quantize_a_pos(2)
+        nxt = seconds(0, FILL[0])
         first(2)
-        turn_a(2, (4, 5))
         interleave_a(3, SPLIT[3])
+        quantize_a_ch(1)
         quantize_a_pos(3)
         first(3)
-        quantize_a_ch(1)
-        copy_turned(2, 0, False)
-        copy_turned(2, 1, False)
-        nxt = seconds(nxt, FILL[0])
-        interleave_a(4, SPLIT[4])
-        quantize_a_ch(2)
-        quantize_a_pos(4)
-        first(4)
-        interleave_a(5, SPLIT[5])
-        quantize_a_pos(5)
-        nxt = seconds(nxt, FILL[1])
-        first(5)
+        for g in (4, 5):
+            interleave_a(g, SPLIT[g])
+            quantize_a_pos(g)
+            nxt = seconds(nxt, FILL[g - 3])
+            first(g)
         interleave_a(6, SPLIT[6])
-        interleave_a(7, SPLIT[7])
+        if PAIR:
+            interleave_a(7, SPLIT[7])
         quantize_a_pos(6)
-        quantize_a_pos(7)
-        nxt = seconds(nxt, FILL[2])
+        nxt = seconds(nxt, FILL[3])
         first(6)
-        first(7)
+        if not PAIR:
+            interleave_a(7, SPLIT[7])
+        nxt = seconds(nxt, FILL[4])
+        quantize_a_pos_by_slot(7)
         for t in range(PACK):
             weigh_target(0, t, False)
             error(0, t)
-        weigh_target(1, 0, False)
-        weigh_target(1, 1, False)
+        for t in range(W1):
+            weigh_target(1, t, False)
         quantize_error(0, SCALAR_N)
-        weigh_target(1, 2, False)
-        weigh_target(1, 3, False)
-        nxt = seconds(nxt, FILL[4])
+        for t in range(W1, PACK):
+            weigh_target(1, t, W1V)
+        nxt = seconds(nxt, FILL[5])
 
         for n in range(EARLY * PACK):
             g, j = divmod(n, PACK)
-            half_tile(g, j, 0, n % 4, n in VT, 1 if n < 2 else 2)
-            nxt = seconds(nxt, PER[min(n, len(PER) - 1)])
+            half_tile(g, j, 0, n % 4, n in VT, 1 if n < 2 else (2 if n < 4 else PS))
+            nxt = seconds(nxt, PER)
             for t in range(PACK):
                 if ER[t] == n:
                     error(1, t)
-            if n == TR3:
-                turn_a(3, (4, 5) if TR3 < 11 else (6, 7))
+            if n == TR2:
+                turn_a(EARLY, (4, 5))
             if n == QE1:
                 quantize_error(1, SN1)
-        nxt_g = 3
 
         n = 0
         for k in range(EARLY):
             for j in range(PACK):
-                half_tile(k, j, 1, n % 4, n % 2 == 1, 2)
+                half_tile(k, j, 1, n % 4, n % 2 == 1, PS)
                 n = n + 1
                 if k == 0 and j < 2:
-                    copy_turned(nxt_g, j, j == 0)
+                    copy_turned(EARLY, j, j == 0)
                 if k == 0 and j == 3:
-                    quantize_a_ch(nxt_g)
+                    quantize_a_ch(EARLY)
         for g in range(EARLY, GROUPS):
-            ahead = g + 1 if g + 1 < GROUPS else None
+            ahead = g + 1 < GROUPS
             if ahead:
-                turn_a(ahead, (6, 7))
+                turn_a(g + 1, (6, 7))
             for j in range(PACK):
                 for h in range(2):
-                    full_tile(g, j, h, n % 6, n % 2 == 1, 1 if g == GROUPS - 1 else 2)
+                    full_tile(g, j, h, n % 6, n % 2 == 1, 2)
                     n = n + 1
                 if ahead and j < 2:
-                    copy_turned(ahead, j, j == 1)
+                    copy_turned(g + 1, j, j == 1)
                 if ahead and j == 2:
-                    quantize_a_ch(ahead)
+                    quantize_a_ch(g + 1)

@@ -3,8 +3,8 @@ from contextlib import ExitStack
 import concourse.mybir as mybir
 from concourse.masks import make_identity
 
-POS, CH, OUT = 4096, 512, 1024
-FLOPS = 2 * 2 * POS * CH * OUT
+POSITIONS, CHANNELS, COLUMNS = 4096, 512, 1024
+FLOPS = 2 * 2 * POSITIONS * CHANNELS * COLUMNS
 
 F32 = mybir.dt.float32
 BF16 = mybir.dt.bfloat16
@@ -15,27 +15,22 @@ E4M3 = mybir.dt.float8_e4m3fn_x4
 E5M2 = mybir.dt.float8_e5m2_x4
 E2M1 = mybir.dt.float4_e2m1fn_x4
 ALU = mybir.AluOpType
-ACT = mybir.ActivationFunctionType
+COPY = mybir.ActivationFunctionType.Copy
 
 P = 128
-PACK = 4
-GROUP = P * PACK
-GROUPS = POS // GROUP
-HALF = 512
-SPLIT = [44,44,60,60,60,44,44,60]
-FILL = [4,6,0,3,0,14]
-PAIR = False
-W1 = 0
-W1V = True
-PER = 1
-ER = [0,1,2,4]
-VT = []
-TR2 = 5
-QE1 = 4
-SN1 = 96
-EARLY = 2
-PS = 2
-SCALAR_N = 176
+SLOTS = 4
+PASS = P * SLOTS
+GROUPS = POSITIONS // PASS
+HALF = COLUMNS // 2
+WEIGHT_ROW = GROUPS
+EARLY = 3
+
+SCALAR_A = 60
+SCALAR_A_FIRST = 44
+SCALAR_A_LAST = 76
+SCALAR_E = (176, 96)
+BETWEEN = {5: 1, 6: 2}
+AHEAD = 15
 
 
 def tile_cross_gram_texture_gradient_s9_kernel(tc, a, b_words, b_scales, target, weight, guide, out):
@@ -50,291 +45,285 @@ def tile_cross_gram_texture_gradient_s9_kernel(tc, a, b_words, b_scales, target,
         def bank(i):
             return psum.tile([P, HALF], F32, name="bank%d" % i)
 
-        raw, b_code, b_scale, tgt, wtgt = {}, {}, {}, {}, {}
-        a_pos, a_pos_q, turned, a_ch, a_ch_q = {}, {}, {}, {}, {}
-        gram, err, err_q, result, closed = {}, {}, {}, {}, {}
+        raw, b_code, b_scale, tgt, weighted = {}, {}, {}, {}, {}
+        by_position, by_position_mx, turned, by_channel, by_channel_mx = {}, {}, {}, {}, {}
+        gram, err, err_mx, result = {}, {}, {}, {}
 
         ident = keep.tile([P, P], F32, name="ident")
-        rows = keep.tile([P, GROUP], BF16, name="rows")
-        cols = keep.tile([P, GROUPS + 1, PACK], F32, name="cols")
+        vector_rows = keep.tile([P, PASS], BF16, name="rows")
+        vectors = keep.tile([P, GROUPS + 1, SLOTS], F32, name="vectors")
 
         def load_a(g):
-            raw[g] = keep.tile([P, PACK, CH], BF16, name="raw%d" % g, align_bytes=64)
-            nc.sync.dma_start(out=raw[g][:], in_=a[g * GROUP:(g + 1) * GROUP, :].rearrange("(p j) c -> p j c", j=PACK))
+            raw[g] = keep.tile([P, SLOTS, CHANNELS], BF16, name="raw%d" % g, align_bytes=64)
+            nc.sync.dma_start(out=raw[g][:], in_=a[g * PASS:(g + 1) * PASS, :].rearrange("(p j) c -> p j c", j=SLOTS))
 
-        def load_b(g0, n, h0, halves):
-            t = keep.tile([P, n, halves * 2 * HALF], U8, name="bw%d_%d" % (g0, h0), align_bytes=64)
-            src = b_words[g0:g0 + n, :, 2 * HALF * h0:2 * HALF * (h0 + halves)].rearrange("g p n -> p g n")
-            nc.sync.dma_start(out=t[:].bitcast(I32), in_=src.bitcast(I32))
-            for i in range(n):
-                for h in range(halves):
-                    b_code[h0 + h, g0 + i] = t[:, i, 2 * HALF * h:2 * HALF * (h + 1)]
+        def load_b(groups, halves):
+            width = 2 * HALF
+            tile = keep.tile([P, len(groups), len(halves) * width], U8, name="bw%d_%d" % (groups[0], halves[0]), align_bytes=64)
+            src = b_words[groups[0]:groups[-1] + 1, :, width * halves[0]:width * (halves[-1] + 1)]
+            nc.sync.dma_start(out=tile[:].bitcast(I32), in_=src.rearrange("g p n -> p g n").bitcast(I32))
+            for i, g in enumerate(groups):
+                for k, h in enumerate(halves):
+                    b_code[h, g] = tile[:, i, width * k:width * (k + 1)]
 
-        def clear_scales(s, engine):
-            b_scale[s] = keep.tile([P, 4, OUT], U8, name="bs%d" % s, align_bytes=64)
-            engine.memset(b_scale[s][:].bitcast(I32), 0)
+        def clear_scales(s):
+            b_scale[s] = keep.tile([P, 4, COLUMNS], U8, name="bs%d" % s, align_bytes=64)
+            nc.vector.memset(b_scale[s][:].bitcast(I32), 0)
 
         def load_scales(s):
             for r in range(4):
                 src = b_scales[4 * s:4 * s + 4, r:16:4, :].rearrange("g q n -> q g n")
                 nc.sync.dma_start(out=b_scale[s][r:P:32, :, :].bitcast(I32), in_=src.bitcast(I32))
 
-        def load_target(h, t0, n):
-            tile = keep.tile([P, n, HALF], BF16, name="tgt%d_%d" % (h, t0))
-            src = target[:, HALF * h:HALF * (h + 1)].rearrange("(p t) n -> p t n", t=PACK)
-            nc.sync.dma_start(out=tile[:], in_=src[:, t0:t0 + n, :])
-            for i in range(n):
-                tgt[h, t0 + i] = tile[:, i, :]
+        def load_vectors():
+            nc.sync.dma_start(out=vector_rows[0:GROUPS, :], in_=guide.rearrange("(g c) -> g c", g=GROUPS))
+            nc.sync.dma_start(out=vector_rows[WEIGHT_ROW:WEIGHT_ROW + 1, :], in_=weight.rearrange("(g c) -> g c", g=1))
+
+        def load_target(h, slots):
+            tile = keep.tile([P, len(slots), HALF], BF16, name="tgt%d_%d" % (h, slots[0]))
+            src = target[:, HALF * h:HALF * (h + 1)].rearrange("(p t) n -> p t n", t=SLOTS)
+            nc.sync.dma_start(out=tile[:], in_=src[:, slots[0]:slots[-1] + 1, :])
+            for i, t in enumerate(slots):
+                tgt[h, t] = tile[:, i, :]
+
+        def turn_row(dst, words):
+            for u in range(2):
+                nc.tensor.transpose(out=dst[:, u * P:(u + 1) * P], in_=words[:, u:2 * P:2], identity=ident[:])
 
         def turn_vectors(bk):
-            pt = bank(bk)
-            words = rows[:].bitcast(F32)
-            for u in range(2):
-                nc.tensor.transpose(out=pt[:, u * P:(u + 1) * P], in_=words[:, u:2 * P:2], identity=ident[:])
-            turned["vectors"] = pt
+            turned["vectors"] = bank(bk)
+            turn_row(turned["vectors"][:, 0:2 * P], vector_rows[:].bitcast(F32))
 
         def copy_vectors():
-            pt = turned["vectors"]
-            view = pt[:, 0:2 * P].bitcast(BF16).rearrange("p (u r e) -> p r u e", u=2, e=2)
-            nc.vector.tensor_copy(out=cols[:].rearrange("p r (u e) -> p r u e", u=2), in_=view[:, 0:GROUPS + 1, :, :])
-
-        def interleave_a(g, split):
-            a_pos[g] = stage.tile([P, PACK, P, PACK], BF16, name="a_pos", align_bytes=64)
-            dst = a_pos[g][:].rearrange("p t (b m) j -> p b t m j", m=2)
-            src = raw[g][:].rearrange("p j (b m t) -> p b t m j", m=2, t=PACK)
-            nc.vector.tensor_copy(out=dst[:, split // 2:], in_=src[:, split // 2:])
-            nc.scalar.copy(out=dst[:, 0:split // 2], in_=src[:, 0:split // 2])
-
-        def quantize(name, src, fmt):
-            width = src.shape[1] // PACK
-            codes = keep.tile([P, width], U32, name="c_" + name, align_bytes=64)
-            scales = keep.tile([P, width], U8, name="s_" + name, align_bytes=64)
-            nc.vector.quantize_mx(out=codes[:].bitcast(fmt), scales=scales[:], in_=src)
-            return codes, scales
-
-        def quantize_a_pos(g):
-            a_pos_q[g] = quantize("ap%d" % g, a_pos[g][:].rearrange("p t m j -> p (t m j)"), E4M3)
-
-        def quantize_a_pos_by_slot(g):
-            codes = keep.tile([P, GROUP], U32, name="c_ap%d" % g, align_bytes=64)
-            scales = keep.tile([P, GROUP], U8, name="s_ap%d" % g, align_bytes=64)
-            a_pos_q[g] = codes, scales
-            for t in range(PACK):
-                nc.vector.quantize_mx(
-                    out=codes[:, t * P:(t + 1) * P].bitcast(E4M3), scales=scales[:, t * P:(t + 1) * P],
-                    in_=a_pos[g][:, t, :, :].rearrange("p m j -> p (m j)"))
-                gram_pass(0, t, g, t)
-
-        def gram_pass(h, t, g, bk):
-            if g == 0:
-                gram[h, t] = bank(bk)
-            closed[h, t] = g == GROUPS - 1
-            codes, scales = a_pos_q[g]
-            nc.tensor.matmul_mx(
-                out=gram[h, t][:], lhsT=codes[:, t * P:(t + 1) * P].bitcast(E4M3), lhsT_scale=scales[:, t * P:(t + 1) * P],
-                rhs=b_code[h, g].bitcast(E2M1), rhs_scale=b_scale[g // 4][:, g % 4, HALF * h:HALF * (h + 1)], start=(g == 0), stop=(g == GROUPS - 1))
+            view = turned["vectors"][:, 0:2 * P].bitcast(BF16).rearrange("p (u r e) -> p r u e", u=2, e=2)
+            nc.vector.tensor_copy(out=vectors[:].rearrange("p r (u e) -> p r u e", u=2), in_=view[:, 0:GROUPS + 1, :, :])
 
         def turn_a(g, banks):
             words = raw[g][:].rearrange("p j c -> p (j c)").bitcast(F32)
             for s in range(2):
                 turned[g, s] = bank(banks[s])
-                for jj in range(2):
-                    for u in range(2):
-                        w0 = (2 * s + jj) * 2 * P + u
-                        c0 = (2 * jj + u) * P
-                        nc.tensor.transpose(out=turned[g, s][:, c0:c0 + P], in_=words[:, w0:w0 + 2 * P - u:2], identity=ident[:])
+                for i in range(2):
+                    j = 2 * s + i
+                    turn_row(turned[g, s][:, 2 * P * i:2 * P * (i + 1)], words[:, 2 * P * j:2 * P * (j + 1)])
 
         def copy_turned(g, s, on_vector):
             if s == 0:
-                a_ch[g] = stage.tile([P, 2, 2 * P * 2], F32, name="a_ch", align_bytes=64)
-            dst = a_ch[g][:, s, :].rearrange("p (j r u) -> p j r u", j=2, u=2)
-            src = turned[g, s][:].rearrange("p (j u r) -> p j r u", j=2, u=2)
+                by_channel[g] = stage.tile([P, 2, HALF], F32, name="a_ch", align_bytes=64)
+            dst = by_channel[g][:, s, :].rearrange("p (i r u) -> p i r u", i=2, u=2)
+            src = turned[g, s][:].rearrange("p (i u r) -> p i r u", i=2, u=2)
             if on_vector:
                 nc.vector.tensor_copy(out=dst, in_=src)
             else:
                 nc.scalar.copy(out=dst, in_=src)
 
-        def quantize_a_ch(g):
-            a_ch_q[g] = quantize("ac%d" % g, a_ch[g][:].rearrange("p s w -> p (s w)").bitcast(BF16), E4M3)
+        def mx_tiles(name):
+            codes = keep.tile([P, PASS], U32, name="c_" + name, align_bytes=64)
+            scales = keep.tile([P, PASS], U8, name="s_" + name, align_bytes=64)
+            return codes, scales
+
+        def quantize(name, src, fmt):
+            codes, scales = mx_tiles(name)
+            nc.vector.quantize_mx(out=codes[:].bitcast(fmt), scales=scales[:], in_=src)
+            return codes, scales
+
+        def interleave_a(g):
+            by_position[g] = stage.tile([P, SLOTS, P, SLOTS], BF16, name="a_pos", align_bytes=64)
+            dst = by_position[g][:].rearrange("p t (b m) j -> p b t m j", m=2)
+            src = raw[g][:].rearrange("p j (b m t) -> p b t m j", m=2, t=SLOTS)
+            cut = {0: SCALAR_A_FIRST, GROUPS - 1: SCALAR_A_LAST}.get(g, SCALAR_A) // 2
+            nc.vector.tensor_copy(out=dst[:, cut:], in_=src[:, cut:])
+            nc.scalar.copy(out=dst[:, 0:cut], in_=src[:, 0:cut])
+
+        def quantize_by_position(g):
+            by_position_mx[g] = quantize("ap%d" % g, by_position[g][:].rearrange("p t m j -> p (t m j)"), E4M3)
+
+        def quantize_by_channel(g):
+            by_channel_mx[g] = quantize("ac%d" % g, by_channel[g][:].rearrange("p s w -> p (s w)").bitcast(BF16), E4M3)
+
+        def gram_pass(h, t, g):
+            if g == 0:
+                gram[h, t] = bank(SLOTS * h + t)
+            codes, scales = by_position_mx[g]
+            nc.tensor.matmul_mx(
+                out=gram[h, t][:],
+                lhsT=codes[:, t * P:(t + 1) * P].bitcast(E4M3), lhsT_scale=scales[:, t * P:(t + 1) * P],
+                rhs=b_code[h, g].bitcast(E2M1), rhs_scale=b_scale[g // 4][:, g % 4, HALF * h:HALF * (h + 1)],
+                start=(g == 0), stop=(g == GROUPS - 1))
+
+        def first_half(g):
+            for t in range(SLOTS):
+                gram_pass(0, t, g)
 
         def weigh_target(h, t, on_vector):
             if t == 0:
-                wtgt[h] = keep.tile([P, PACK, HALF], F32, name="wtgt%d" % h)
-            if on_vector == 2:
-                nc.gpsimd.tensor_scalar(out=wtgt[h][:, t, :], in0=tgt[h, t], scalar1=cols[:, GROUPS, t:t + 1],
-                                        scalar2=0.0, op0=ALU.mult, op1=ALU.add)
-            elif on_vector:
-                nc.vector.tensor_scalar_mul(out=wtgt[h][:, t, :], in0=tgt[h, t], scalar1=cols[:, GROUPS, t:t + 1])
+                weighted[h] = keep.tile([P, SLOTS, HALF], F32, name="wtgt%d" % h)
+            w = vectors[:, WEIGHT_ROW, t:t + 1]
+            if on_vector:
+                nc.vector.tensor_scalar_mul(out=weighted[h][:, t, :], in0=tgt[h, t], scalar1=w)
             else:
-                nc.scalar.activation(out=wtgt[h][:, t, :], in_=tgt[h, t], func=ACT.Copy, scale=cols[:, GROUPS, t:t + 1])
+                nc.scalar.activation(out=weighted[h][:, t, :], in_=tgt[h, t], func=COPY, scale=w)
 
         def error(h, t):
-            assert closed[h, t]
-            closed["e", h, t] = True
             if t == 0:
-                err[h] = keep.tile([P, PACK, HALF], BF16, name="err%d" % h)
+                err[h] = keep.tile([P, SLOTS, HALF], BF16, name="err%d" % h)
             nc.vector.scalar_tensor_tensor(
-                out=err[h][:, t, :], in0=gram[h, t][:], scalar=cols[:, GROUPS, t:t + 1], in1=wtgt[h][:, t, :],
+                out=err[h][:, t, :], in0=gram[h, t][:], scalar=vectors[:, WEIGHT_ROW, t:t + 1], in1=weighted[h][:, t, :],
                 op0=ALU.mult, op1=ALU.subtract)
 
-        def quantize_error(h, scalar_n):
-            assert all(closed["e", h, t] for t in range(PACK))
-            grouped = keep.tile([P, HALF, PACK], BF16, name="eg%d" % h, align_bytes=64)
+        def quantize_error(h):
+            grouped = keep.tile([P, HALF, SLOTS], BF16, name="eg%d" % h, align_bytes=64)
             dst = grouped[:].rearrange("p (c i) t -> p c t i", i=4)
             src = err[h][:].rearrange("p t (c i) -> p c t i", i=4)
-            split = scalar_n // 4
-            nc.vector.tensor_copy(out=dst[:, split:], in_=src[:, split:])
-            if split:
-                nc.scalar.copy(out=dst[:, 0:split], in_=src[:, 0:split])
-            err_q[h] = quantize("e%d" % h, grouped[:].rearrange("p n t -> p (n t)"), E5M2)
+            cut = SCALAR_E[h] // 4
+            nc.vector.tensor_copy(out=dst[:, cut:], in_=src[:, cut:])
+            nc.scalar.copy(out=dst[:, 0:cut], in_=src[:, 0:cut])
+            err_mx[h] = quantize("e%d" % h, grouped[:].rearrange("p n t -> p (n t)"), E5M2)
 
         def out_tile(g, j, h, bk, dst, on_vector):
             acc = bank(bk)
-            codes, scales = a_ch_q[g]
-            e_codes, e_scales = err_q[h]
+            codes, scales = by_channel_mx[g]
+            e_codes, e_scales = err_mx[h]
             nc.tensor.matmul_mx(
-                out=acc[:], lhsT=codes[:, j * P:(j + 1) * P].bitcast(E4M3), lhsT_scale=scales[:, j * P:(j + 1) * P],
+                out=acc[:],
+                lhsT=codes[:, j * P:(j + 1) * P].bitcast(E4M3), lhsT_scale=scales[:, j * P:(j + 1) * P],
                 rhs=e_codes[:].bitcast(E5M2), rhs_scale=e_scales[:], start=True, stop=True)
             if on_vector:
-                nc.vector.tensor_scalar_mul(out=dst, in0=acc[:], scalar1=cols[:, g, j:j + 1])
+                nc.vector.tensor_scalar_mul(out=dst, in0=acc[:], scalar1=vectors[:, g, j:j + 1])
             else:
-                nc.scalar.activation(out=dst, in_=acc[:], func=ACT.Copy, scale=cols[:, g, j:j + 1])
+                nc.scalar.activation(out=dst, in_=acc[:], func=COPY, scale=vectors[:, g, j:j + 1])
 
         def out_rows(g):
-            return out[g * GROUP:(g + 1) * GROUP, :].rearrange("(p j) n -> p j n", j=PACK)
+            return out[g * PASS:(g + 1) * PASS, :].rearrange("(p j) n -> p j n", j=SLOTS)
 
         def half_tile(g, j, h, bk, on_vector, per_store):
             if j == 0:
-                result[g, h] = outs.tile([P, PACK, HALF], F32, name="result")
-            out_tile(g, j, h, bk, result[g, h][:, j, :], on_vector)
+                result[g] = outs.tile([P, SLOTS, HALF], F32, name="result")
+            out_tile(g, j, h, bk, result[g][:, j, :], on_vector)
             if (j + 1) % per_store == 0:
                 js = slice(j + 1 - per_store, j + 1)
-                nc.sync.dma_start(out=out_rows(g)[:, js, HALF * h:HALF * (h + 1)], in_=result[g, h][:, js, :])
+                nc.sync.dma_start(out=out_rows(g)[:, js, HALF * h:HALF * (h + 1)], in_=result[g][:, js, :])
 
-        def full_tile(g, j, h, bk, on_vector, per_store):
-            if j % 2 == 0 and h == 0:
-                result[g, j // 2] = outs.tile([P, 2, OUT], F32, name="result")
-            out_tile(g, j, h, bk, result[g, j // 2][:, j % 2, HALF * h:HALF * (h + 1)], on_vector)
-            if (j + 1) % per_store == 0 and h == 1:
-                j0 = j + 1 - per_store
-                nc.sync.dma_start(out=out_rows(g)[:, j0:j + 1, :], in_=result[g, j // 2][:, j0 % 2:j % 2 + 1, :])
+        def row_pair(g, j0, n0):
+            pair = outs.tile([P, 2, COLUMNS], F32, name="result")
+            for n in range(4):
+                i, h = divmod(n, 2)
+                out_tile(g, j0 + i, h, (n0 + n) % 6, pair[:, i, HALF * h:HALF * (h + 1)], on_vector=(h == 1))
+            nc.sync.dma_start(out=out_rows(g)[:, j0:j0 + 2, :], in_=pair[:])
 
-        nc.vector.memset(rows[:].bitcast(I32), 0)
-        clear_scales(0, nc.vector)
+        clear_scales(0)
+        nc.vector.memset(vector_rows[:].bitcast(I32), 0)
+        clear_scales(1)
         make_identity(nc, ident[:])
-        clear_scales(1, nc.gpsimd)
+
         load_a(0)
-        nc.scalar.dma_start(out=rows[0:GROUPS, :], in_=guide.rearrange("(g c) -> g c", g=GROUPS))
-        nc.scalar.dma_start(out=rows[GROUPS:GROUPS + 1, :], in_=weight.rearrange("(g c) -> g c", g=1))
         load_scales(0)
-        load_b(0, 1, 0, 2)
+        load_b([0], [0, 1])
         load_a(1)
-        load_b(1, 1, 0, 2)
+        load_vectors()
+        load_b([1], [0, 1])
         load_a(2)
         load_a(3)
-        load_b(2, 2, 0, 2)
+        load_b([2, 3], [0])
         load_a(4)
         load_scales(1)
         load_a(5)
-        load_b(4, 2, 0, 1)
+        load_b([4, 5], [0])
         load_a(6)
         load_a(7)
-        load_b(6, 2, 0, 1)
-        load_target(0, 0, 2)
-        load_target(0, 2, 2)
-        load_b(4, 4, 1, 1)
-        load_target(1, 0, 4)
+        load_b([6, 7], [0])
+        load_target(0, [0, 1])
+        load_target(0, [2, 3])
+        load_b([2, 3, 4, 5], [1])
+        load_target(1, [0, 1, 2, 3])
+        load_b([6, 7], [1])
 
-        fill = [(t, g) for g in range(4) for t in range(PACK)] + [(t, g) for t in range(PACK) for g in range(4, GROUPS)]
+        second = [(t, g) for g in range(GROUPS - 2) for t in (2, 3, 0, 1)]
+        second = second + [(t, g) for t in range(SLOTS) for g in (GROUPS - 2, GROUPS - 1)]
 
-        def first(g):
-            for t in range(PACK):
-                gram_pass(0, t, g, t)
+        def second_half(start, count):
+            for t, g in second[start:start + count]:
+                gram_pass(1, t, g)
+                if g == GROUPS - 1:
+                    error(1, t)
+            return start + count
 
-        def seconds(start, count):
-            stop = min(start + count, len(fill))
-            for t, g in fill[start:stop]:
-                gram_pass(1, t, g, 4 + t)
-            return stop
-
-        turn_vectors(3)
         turn_a(0, (4, 5))
-        interleave_a(0, SPLIT[0])
-        copy_vectors()
-        quantize_a_pos(0)
+        interleave_a(0)
+        quantize_by_position(0)
         copy_turned(0, 0, True)
         copy_turned(0, 1, False)
-        first(0)
+        first_half(0)
         turn_a(1, (6, 7))
-        interleave_a(1, SPLIT[1])
-        quantize_a_ch(0)
-        quantize_a_pos(1)
-        first(1)
-        interleave_a(2, SPLIT[2])
+        turn_vectors(4)
+        interleave_a(1)
+        quantize_by_channel(0)
+        quantize_by_position(1)
+        first_half(1)
+        interleave_a(2)
+        copy_vectors()
         copy_turned(1, 0, True)
         copy_turned(1, 1, False)
-        quantize_a_pos(2)
-        nxt = seconds(0, FILL[0])
-        first(2)
-        interleave_a(3, SPLIT[3])
-        quantize_a_ch(1)
-        quantize_a_pos(3)
-        first(3)
-        for g in (4, 5):
-            interleave_a(g, SPLIT[g])
-            quantize_a_pos(g)
-            nxt = seconds(nxt, FILL[g - 3])
-            first(g)
-        interleave_a(6, SPLIT[6])
-        if PAIR:
-            interleave_a(7, SPLIT[7])
-        quantize_a_pos(6)
-        nxt = seconds(nxt, FILL[3])
-        first(6)
-        if not PAIR:
-            interleave_a(7, SPLIT[7])
-        nxt = seconds(nxt, FILL[4])
-        quantize_a_pos_by_slot(7)
-        for t in range(PACK):
+        quantize_by_position(2)
+        turn_a(2, (4, 5))
+        first_half(2)
+        interleave_a(3)
+        quantize_by_channel(1)
+        quantize_by_position(3)
+        first_half(3)
+        copy_turned(2, 0, False)
+        copy_turned(2, 1, False)
+
+        interleave_a(4)
+        quantize_by_channel(2)
+        quantize_by_position(4)
+        done = second_half(0, SLOTS)
+        first_half(4)
+        for g in (5, 6):
+            interleave_a(g)
+            quantize_by_position(g)
+            done = second_half(done, BETWEEN[g])
+            first_half(g)
+
+        last = GROUPS - 1
+        interleave_a(last)
+        by_position_mx[last] = mx_tiles("ap%d" % last)
+        for t in range(SLOTS):
+            codes, scales = by_position_mx[last]
+            nc.vector.quantize_mx(
+                out=codes[:, t * P:(t + 1) * P].bitcast(E4M3), scales=scales[:, t * P:(t + 1) * P],
+                in_=by_position[last][:, t, :, :].rearrange("p m j -> p (m j)"))
+            gram_pass(0, t, last)
+        for t in range(SLOTS):
             weigh_target(0, t, False)
             error(0, t)
-        for t in range(W1):
-            weigh_target(1, t, False)
-        quantize_error(0, SCALAR_N)
-        for t in range(W1, PACK):
-            weigh_target(1, t, W1V)
-        nxt = seconds(nxt, FILL[5])
+        quantize_error(0)
+        for t in range(SLOTS):
+            weigh_target(1, t, on_vector=(t >= 2))
+        done = second_half(done, AHEAD)
 
-        for n in range(EARLY * PACK):
-            g, j = divmod(n, PACK)
-            half_tile(g, j, 0, n % 4, n in VT, 1 if n < 2 else (2 if n < 4 else PS))
-            nxt = seconds(nxt, PER)
-            for t in range(PACK):
-                if ER[t] == n:
-                    error(1, t)
-            if n == TR2:
+        for n in range(EARLY * SLOTS):
+            g, j = divmod(n, SLOTS)
+            half_tile(g, j, 0, n % 4, on_vector=(n in (1, 3)), per_store=(1 if n < 2 else 2))
+            if done == len(second):
+                quantize_error(1)
+            done = second_half(done, 2 if n < 2 else 1)
+            if n == EARLY * SLOTS - 2:
                 turn_a(EARLY, (4, 5))
-            if n == QE1:
-                quantize_error(1, SN1)
 
-        n = 0
-        for k in range(EARLY):
-            for j in range(PACK):
-                half_tile(k, j, 1, n % 4, n % 2 == 1, PS)
-                n = n + 1
-                if k == 0 and j < 2:
-                    copy_turned(EARLY, j, j == 0)
-                if k == 0 and j == 3:
-                    quantize_a_ch(EARLY)
+        for n in range(EARLY * SLOTS):
+            g, j = divmod(n, SLOTS)
+            half_tile(g, j, 1, n % 4, on_vector=(n % 2 == 1), per_store=2)
+            if n < 2:
+                copy_turned(EARLY, n, on_vector=(n == 0))
+            if n == SLOTS:
+                quantize_by_channel(EARLY)
+
         for g in range(EARLY, GROUPS):
-            ahead = g + 1 < GROUPS
-            if ahead:
+            if g < last:
                 turn_a(g + 1, (6, 7))
-            for j in range(PACK):
-                for h in range(2):
-                    full_tile(g, j, h, n % 6, n % 2 == 1, 2)
-                    n = n + 1
-                if ahead and j < 2:
-                    copy_turned(g + 1, j, j == 1)
-                if ahead and j == 2:
-                    quantize_a_ch(g + 1)
+                copy_turned(g + 1, 0, False)
+                copy_turned(g + 1, 1, True)
+            row_pair(g, 0, 8 * g)
+            if g < last:
+                quantize_by_channel(g + 1)
+            row_pair(g, 2, 8 * g + 4)

@@ -23,14 +23,12 @@ PASS = P * SLOTS
 GROUPS = POSITIONS // PASS
 HALF = COLUMNS // 2
 WEIGHT_ROW = GROUPS
-EARLY = 3
+EARLY = 2
 
 SCALAR_A = 60
-SCALAR_A_FIRST = 44
-SCALAR_A_LAST = 76
-SCALAR_E = (176, 96)
-BETWEEN = {5: 1, 6: 2}
-AHEAD = 15
+SCALAR_A_FREE = 44
+SCALAR_A_LAST = 68
+SCALAR_E = 176
 
 
 def tile_cross_gram_texture_gradient_s9_kernel(tc, a, b_words, b_scales, target, weight, guide, out):
@@ -38,7 +36,7 @@ def tile_cross_gram_texture_gradient_s9_kernel(tc, a, b_words, b_scales, target,
     with ExitStack() as ctx:
         keep = ctx.enter_context(tc.tile_pool(name="keep", bufs=1))
         stage = ctx.enter_context(tc.tile_pool(name="stage", bufs=3))
-        outs = ctx.enter_context(tc.tile_pool(name="outs", bufs=8))
+        outs = ctx.enter_context(tc.tile_pool(name="outs", bufs=4))
         psum = ctx.enter_context(tc.psum_pool(name="psum", bufs=1))
         ctx.enter_context(tc.manual_schedule())
 
@@ -79,12 +77,13 @@ def tile_cross_gram_texture_gradient_s9_kernel(tc, a, b_words, b_scales, target,
             nc.sync.dma_start(out=vector_rows[0:GROUPS, :], in_=guide.rearrange("(g c) -> g c", g=GROUPS))
             nc.sync.dma_start(out=vector_rows[WEIGHT_ROW:WEIGHT_ROW + 1, :], in_=weight.rearrange("(g c) -> g c", g=1))
 
-        def load_target(h, slots):
-            tile = keep.tile([P, len(slots), HALF], BF16, name="tgt%d_%d" % (h, slots[0]))
+        def load_target(h):
             src = target[:, HALF * h:HALF * (h + 1)].rearrange("(p t) n -> p t n", t=SLOTS)
-            nc.sync.dma_start(out=tile[:], in_=src[:, slots[0]:slots[-1] + 1, :])
-            for i, t in enumerate(slots):
-                tgt[h, t] = tile[:, i, :]
+            for t0 in (0, 2):
+                tile = keep.tile([P, 2, HALF], BF16, name="tgt%d_%d" % (h, t0))
+                nc.sync.dma_start(out=tile[:], in_=src[:, t0:t0 + 2, :])
+                for i in range(2):
+                    tgt[h, t0 + i] = tile[:, i, :]
 
         def turn_row(dst, words):
             for u in range(2):
@@ -126,11 +125,11 @@ def tile_cross_gram_texture_gradient_s9_kernel(tc, a, b_words, b_scales, target,
             nc.vector.quantize_mx(out=codes[:].bitcast(fmt), scales=scales[:], in_=src)
             return codes, scales
 
-        def interleave_a(g):
+        def interleave_a(g, scalar_columns):
             by_position[g] = stage.tile([P, SLOTS, P, SLOTS], BF16, name="a_pos", align_bytes=64)
             dst = by_position[g][:].rearrange("p t (b m) j -> p b t m j", m=2)
             src = raw[g][:].rearrange("p j (b m t) -> p b t m j", m=2, t=SLOTS)
-            cut = {0: SCALAR_A_FIRST, GROUPS - 1: SCALAR_A_LAST}.get(g, SCALAR_A) // 2
+            cut = scalar_columns // 2
             nc.vector.tensor_copy(out=dst[:, cut:], in_=src[:, cut:])
             nc.scalar.copy(out=dst[:, 0:cut], in_=src[:, 0:cut])
 
@@ -150,18 +149,14 @@ def tile_cross_gram_texture_gradient_s9_kernel(tc, a, b_words, b_scales, target,
                 rhs=b_code[h, g].bitcast(E2M1), rhs_scale=b_scale[g // 4][:, g % 4, HALF * h:HALF * (h + 1)],
                 start=(g == 0), stop=(g == GROUPS - 1))
 
-        def first_half(g):
+        def gram_group(h, g):
             for t in range(SLOTS):
-                gram_pass(0, t, g)
+                gram_pass(h, t, g)
 
-        def weigh_target(h, t, on_vector):
+        def weigh_target(h, t):
             if t == 0:
                 weighted[h] = keep.tile([P, SLOTS, HALF], F32, name="wtgt%d" % h)
-            w = vectors[:, WEIGHT_ROW, t:t + 1]
-            if on_vector:
-                nc.vector.tensor_scalar_mul(out=weighted[h][:, t, :], in0=tgt[h, t], scalar1=w)
-            else:
-                nc.scalar.activation(out=weighted[h][:, t, :], in_=tgt[h, t], func=COPY, scale=w)
+            nc.scalar.activation(out=weighted[h][:, t, :], in_=tgt[h, t], func=COPY, scale=vectors[:, WEIGHT_ROW, t:t + 1])
 
         def error(h, t):
             if t == 0:
@@ -170,16 +165,19 @@ def tile_cross_gram_texture_gradient_s9_kernel(tc, a, b_words, b_scales, target,
                 out=err[h][:, t, :], in0=gram[h, t][:], scalar=vectors[:, WEIGHT_ROW, t:t + 1], in1=weighted[h][:, t, :],
                 op0=ALU.mult, op1=ALU.subtract)
 
-        def quantize_error(h):
+        def quantize_error(h, scalar_columns):
             grouped = keep.tile([P, HALF, SLOTS], BF16, name="eg%d" % h, align_bytes=64)
             dst = grouped[:].rearrange("p (c i) t -> p c t i", i=4)
             src = err[h][:].rearrange("p t (c i) -> p c t i", i=4)
-            cut = SCALAR_E[h] // 4
+            cut = scalar_columns // 4
             nc.vector.tensor_copy(out=dst[:, cut:], in_=src[:, cut:])
-            nc.scalar.copy(out=dst[:, 0:cut], in_=src[:, 0:cut])
+            if cut:
+                nc.scalar.copy(out=dst[:, 0:cut], in_=src[:, 0:cut])
             err_mx[h] = quantize("e%d" % h, grouped[:].rearrange("p n t -> p (n t)"), E5M2)
 
-        def out_tile(g, j, h, bk, dst, on_vector):
+        def out_tile(g, j, h, bk, on_vector):
+            if j == 0 and h == 0:
+                result[g] = outs.tile([P, SLOTS, COLUMNS], F32, name="result")
             acc = bank(bk)
             codes, scales = by_channel_mx[g]
             e_codes, e_scales = err_mx[h]
@@ -187,28 +185,20 @@ def tile_cross_gram_texture_gradient_s9_kernel(tc, a, b_words, b_scales, target,
                 out=acc[:],
                 lhsT=codes[:, j * P:(j + 1) * P].bitcast(E4M3), lhsT_scale=scales[:, j * P:(j + 1) * P],
                 rhs=e_codes[:].bitcast(E5M2), rhs_scale=e_scales[:], start=True, stop=True)
+            dst = result[g][:, j, HALF * h:HALF * (h + 1)]
             if on_vector:
                 nc.vector.tensor_scalar_mul(out=dst, in0=acc[:], scalar1=vectors[:, g, j:j + 1])
             else:
                 nc.scalar.activation(out=dst, in_=acc[:], func=COPY, scale=vectors[:, g, j:j + 1])
 
-        def out_rows(g):
-            return out[g * PASS:(g + 1) * PASS, :].rearrange("(p j) n -> p j n", j=SLOTS)
+        def store(g, js, cols):
+            rows = out[g * PASS:(g + 1) * PASS, :].rearrange("(p j) n -> p j n", j=SLOTS)
+            nc.sync.dma_start(out=rows[:, js, cols], in_=result[g][:, js, cols])
 
-        def half_tile(g, j, h, bk, on_vector, per_store):
-            if j == 0:
-                result[g] = outs.tile([P, SLOTS, HALF], F32, name="result")
-            out_tile(g, j, h, bk, result[g][:, j, :], on_vector)
-            if (j + 1) % per_store == 0:
-                js = slice(j + 1 - per_store, j + 1)
-                nc.sync.dma_start(out=out_rows(g)[:, js, HALF * h:HALF * (h + 1)], in_=result[g][:, js, :])
-
-        def row_pair(g, j0, n0):
-            pair = outs.tile([P, 2, COLUMNS], F32, name="result")
-            for n in range(4):
-                i, h = divmod(n, 2)
-                out_tile(g, j0 + i, h, (n0 + n) % 6, pair[:, i, HALF * h:HALF * (h + 1)], on_vector=(h == 1))
-            nc.sync.dma_start(out=out_rows(g)[:, j0:j0 + 2, :], in_=pair[:])
+        def row_pair(g, j0):
+            for j in (j0, j0 + 1):
+                for h in range(2):
+                    out_tile(g, j, h, (8 * g + 2 * j + h) % 6, on_vector=(h == 1))
 
         clear_scales(0)
         nc.vector.memset(vector_rows[:].bitcast(I32), 0)
@@ -223,7 +213,7 @@ def tile_cross_gram_texture_gradient_s9_kernel(tc, a, b_words, b_scales, target,
         load_b([1], [0, 1])
         load_a(2)
         load_a(3)
-        load_b([2, 3], [0])
+        load_b([2, 3], [0, 1])
         load_a(4)
         load_scales(1)
         load_a(5)
@@ -231,61 +221,50 @@ def tile_cross_gram_texture_gradient_s9_kernel(tc, a, b_words, b_scales, target,
         load_a(6)
         load_a(7)
         load_b([6, 7], [0])
-        load_target(0, [0, 1])
-        load_target(0, [2, 3])
-        load_b([2, 3, 4, 5], [1])
-        load_target(1, [0, 1, 2, 3])
-        load_b([6, 7], [1])
-
-        second = [(t, g) for g in range(GROUPS - 2) for t in (2, 3, 0, 1)]
-        second = second + [(t, g) for t in range(SLOTS) for g in (GROUPS - 2, GROUPS - 1)]
-
-        def second_half(start, count):
-            for t, g in second[start:start + count]:
-                gram_pass(1, t, g)
-                if g == GROUPS - 1:
-                    error(1, t)
-            return start + count
+        load_target(0)
+        load_b([4, 5, 6, 7], [1])
+        load_target(1)
 
         turn_a(0, (4, 5))
-        interleave_a(0)
+        interleave_a(0, SCALAR_A_FREE)
         quantize_by_position(0)
         copy_turned(0, 0, True)
         copy_turned(0, 1, False)
-        first_half(0)
+        gram_group(0, 0)
         turn_a(1, (6, 7))
         turn_vectors(4)
-        interleave_a(1)
+        interleave_a(1, SCALAR_A)
         quantize_by_channel(0)
         quantize_by_position(1)
-        first_half(1)
-        interleave_a(2)
+        gram_group(0, 1)
+        interleave_a(2, SCALAR_A)
         copy_vectors()
         copy_turned(1, 0, True)
         copy_turned(1, 1, False)
         quantize_by_position(2)
-        turn_a(2, (4, 5))
-        first_half(2)
-        interleave_a(3)
-        quantize_by_channel(1)
-        quantize_by_position(3)
-        first_half(3)
-        copy_turned(2, 0, False)
-        copy_turned(2, 1, False)
+        gram_group(1, 0)
+        gram_group(0, 2)
 
-        interleave_a(4)
-        quantize_by_channel(2)
+        interleave_a(3, SCALAR_A)
+        quantize_by_position(3)
+        gram_group(1, 1)
+        gram_group(0, 3)
+        interleave_a(4, SCALAR_A)
+        quantize_by_channel(1)
         quantize_by_position(4)
-        done = second_half(0, SLOTS)
-        first_half(4)
-        for g in (5, 6):
-            interleave_a(g)
-            quantize_by_position(g)
-            done = second_half(done, BETWEEN[g])
-            first_half(g)
+        gram_group(1, 2)
+        gram_group(0, 4)
+        interleave_a(5, SCALAR_A_FREE)
+        quantize_by_position(5)
+        gram_group(0, 5)
+        interleave_a(6, SCALAR_A_FREE)
+        quantize_by_position(6)
+        gram_pass(1, 0, 3)
+        gram_pass(1, 1, 3)
+        gram_group(0, 6)
 
         last = GROUPS - 1
-        interleave_a(last)
+        interleave_a(last, SCALAR_A_LAST)
         by_position_mx[last] = mx_tiles("ap%d" % last)
         for t in range(SLOTS):
             codes, scales = by_position_mx[last]
@@ -294,36 +273,59 @@ def tile_cross_gram_texture_gradient_s9_kernel(tc, a, b_words, b_scales, target,
                 in_=by_position[last][:, t, :, :].rearrange("p m j -> p (m j)"))
             gram_pass(0, t, last)
         for t in range(SLOTS):
-            weigh_target(0, t, False)
+            weigh_target(0, t)
             error(0, t)
-        quantize_error(0)
-        for t in range(SLOTS):
-            weigh_target(1, t, on_vector=(t >= 2))
-        done = second_half(done, AHEAD)
+        weigh_target(1, 0)
+        weigh_target(1, 1)
+        quantize_error(0, SCALAR_E)
+        weigh_target(1, 2)
+        weigh_target(1, 3)
+
+        gram_pass(1, 2, 3)
+        gram_pass(1, 3, 3)
+        for t in range(SLOTS - 1):
+            for g in range(4, GROUPS):
+                gram_pass(1, t, g)
+            error(1, t)
+        gram_pass(1, 3, 4)
 
         for n in range(EARLY * SLOTS):
             g, j = divmod(n, SLOTS)
-            half_tile(g, j, 0, n % 4, on_vector=(n in (1, 3)), per_store=(1 if n < 2 else 2))
-            if done == len(second):
-                quantize_error(1)
-            done = second_half(done, 2 if n < 2 else 1)
+            out_tile(g, j, 0, j, on_vector=False)
+            if n < 2:
+                store(g, slice(j, j + 1), slice(0, HALF))
+            elif j % 2 == 1:
+                store(g, slice(j - 1, j + 1), slice(0, HALF))
+            if 5 + n < GROUPS:
+                gram_pass(1, 3, 5 + n)
+            if 5 + n == last:
+                error(1, 3)
+                quantize_error(1, 0)
             if n == EARLY * SLOTS - 2:
                 turn_a(EARLY, (4, 5))
 
         for n in range(EARLY * SLOTS):
             g, j = divmod(n, SLOTS)
-            half_tile(g, j, 1, n % 4, on_vector=(n % 2 == 1), per_store=2)
+            out_tile(g, j, 1, j, on_vector=(j % 2 == 1))
+            if g == 0 and j % 2 == 1:
+                store(g, slice(j - 1, j + 1), slice(HALF, COLUMNS))
+            if g > 0 and j == SLOTS - 1:
+                store(g, slice(0, SLOTS), slice(HALF, COLUMNS))
             if n < 2:
                 copy_turned(EARLY, n, on_vector=(n == 0))
             if n == SLOTS:
                 quantize_by_channel(EARLY)
 
         for g in range(EARLY, GROUPS):
+            in_two = g < EARLY + 2
             if g < last:
                 turn_a(g + 1, (6, 7))
                 copy_turned(g + 1, 0, False)
                 copy_turned(g + 1, 1, True)
-            row_pair(g, 0, 8 * g)
+            row_pair(g, 0)
+            if in_two:
+                store(g, slice(0, 2), slice(0, COLUMNS))
             if g < last:
                 quantize_by_channel(g + 1)
-            row_pair(g, 2, 8 * g + 4)
+            row_pair(g, 2)
+            store(g, slice(2 if in_two else 0, SLOTS), slice(0, COLUMNS))

from contextlib import ExitStack

import concourse.mybir as mybir
from concourse.masks import make_identity

POSITIONS, CHANNELS, COLUMNS = 4096, 512, 1024
FLOPS = 2 * 2 * POSITIONS * CHANNELS * COLUMNS

F32 = mybir.dt.float32
BF16 = mybir.dt.bfloat16
I32 = mybir.dt.int32
U32 = mybir.dt.uint32
U8 = mybir.dt.uint8
E4M3 = mybir.dt.float8_e4m3fn_x4
E5M2 = mybir.dt.float8_e5m2_x4
E2M1 = mybir.dt.float4_e2m1fn_x4
ALU = mybir.AluOpType
COPY = mybir.ActivationFunctionType.Copy

P = 128
SLOTS = 4
PASS = P * SLOTS
GROUPS = POSITIONS // PASS
HALF = COLUMNS // 2
WEIGHT_ROW = GROUPS
EARLY = 2

SCALAR_A = 60
SCALAR_A_FREE = 44
SCALAR_A_LAST = 68
SCALAR_E = 176


def tile_cross_gram_texture_gradient_s9_kernel(tc, a, b_words, b_scales, target, weight, guide, out):
    nc = tc.nc
    with ExitStack() as ctx:
        keep = ctx.enter_context(tc.tile_pool(name="keep", bufs=1))
        stage = ctx.enter_context(tc.tile_pool(name="stage", bufs=3))
        outs = ctx.enter_context(tc.tile_pool(name="outs", bufs=4))
        psum = ctx.enter_context(tc.psum_pool(name="psum", bufs=1))
        ctx.enter_context(tc.manual_schedule())

        def bank(i):
            return psum.tile([P, HALF], F32, name="bank%d" % i)

        raw, b_code, b_scale, tgt, weighted = {}, {}, {}, {}, {}
        by_position, by_position_mx, turned, by_channel, by_channel_mx = {}, {}, {}, {}, {}
        gram, err, err_mx, result = {}, {}, {}, {}

        ident = keep.tile([P, P], F32, name="ident")
        vector_rows = keep.tile([P, PASS], BF16, name="rows")
        vectors = keep.tile([P, GROUPS + 1, SLOTS], F32, name="vectors")

        def load_a(g):
            raw[g] = keep.tile([P, SLOTS, CHANNELS], BF16, name="raw%d" % g, align_bytes=64)
            nc.sync.dma_start(out=raw[g][:], in_=a[g * PASS:(g + 1) * PASS, :].rearrange("(p j) c -> p j c", j=SLOTS))

        def load_b(groups, halves):
            width = 2 * HALF
            tile = keep.tile([P, len(groups), len(halves) * width], U8, name="bw%d_%d" % (groups[0], halves[0]), align_bytes=64)
            src = b_words[groups[0]:groups[-1] + 1, :, width * halves[0]:width * (halves[-1] + 1)]
            nc.sync.dma_start(out=tile[:].bitcast(I32), in_=src.rearrange("g p n -> p g n").bitcast(I32))
            for i, g in enumerate(groups):
                for k, h in enumerate(halves):
                    b_code[h, g] = tile[:, i, width * k:width * (k + 1)]

        def clear_scales(s):
            b_scale[s] = keep.tile([P, 4, COLUMNS], U8, name="bs%d" % s, align_bytes=64)
            nc.vector.memset(b_scale[s][:].bitcast(I32), 0)

        def load_scales(s):
            for r in range(4):
                src = b_scales[4 * s:4 * s + 4, r:16:4, :].rearrange("g q n -> q g n")
                nc.sync.dma_start(out=b_scale[s][r:P:32, :, :].bitcast(I32), in_=src.bitcast(I32))

        def load_vectors():
            nc.sync.dma_start(out=vector_rows[0:GROUPS, :], in_=guide.rearrange("(g c) -> g c", g=GROUPS))
            nc.sync.dma_start(out=vector_rows[WEIGHT_ROW:WEIGHT_ROW + 1, :], in_=weight.rearrange("(g c) -> g c", g=1))

        def load_target(h):
            src = target[:, HALF * h:HALF * (h + 1)].rearrange("(p t) n -> p t n", t=SLOTS)
            for t0 in (0, 2):
                tile = keep.tile([P, 2, HALF], BF16, name="tgt%d_%d" % (h, t0))
                nc.sync.dma_start(out=tile[:], in_=src[:, t0:t0 + 2, :])
                for i in range(2):
                    tgt[h, t0 + i] = tile[:, i, :]

        def turn_row(dst, words):
            for u in range(2):
                nc.tensor.transpose(out=dst[:, u * P:(u + 1) * P], in_=words[:, u:2 * P:2], identity=ident[:])

        def turn_vectors(bk):
            turned["vectors"] = bank(bk)
            turn_row(turned["vectors"][:, 0:2 * P], vector_rows[:].bitcast(F32))

        def copy_vectors():
            view = turned["vectors"][:, 0:2 * P].bitcast(BF16).rearrange("p (u r e) -> p r u e", u=2, e=2)
            nc.vector.tensor_copy(out=vectors[:].rearrange("p r (u e) -> p r u e", u=2), in_=view[:, 0:GROUPS + 1, :, :])

        def turn_a(g, banks):
            words = raw[g][:].rearrange("p j c -> p (j c)").bitcast(F32)
            for s in range(2):
                turned[g, s] = bank(banks[s])
                for i in range(2):
                    j = 2 * s + i
                    turn_row(turned[g, s][:, 2 * P * i:2 * P * (i + 1)], words[:, 2 * P * j:2 * P * (j + 1)])

        def copy_turned(g, s, on_vector):
            if s == 0:
                by_channel[g] = stage.tile([P, 2, HALF], F32, name="a_ch", align_bytes=64)
            dst = by_channel[g][:, s, :].rearrange("p (i r u) -> p i r u", i=2, u=2)
            src = turned[g, s][:].rearrange("p (i u r) -> p i r u", i=2, u=2)
            if on_vector:
                nc.vector.tensor_copy(out=dst, in_=src)
            else:
                nc.scalar.copy(out=dst, in_=src)

        def mx_tiles(name):
            codes = keep.tile([P, PASS], U32, name="c_" + name, align_bytes=64)
            scales = keep.tile([P, PASS], U8, name="s_" + name, align_bytes=64)
            return codes, scales

        def quantize(name, src, fmt):
            codes, scales = mx_tiles(name)
            nc.vector.quantize_mx(out=codes[:].bitcast(fmt), scales=scales[:], in_=src)
            return codes, scales

        def interleave_a(g, scalar_columns):
            by_position[g] = stage.tile([P, SLOTS, P, SLOTS], BF16, name="a_pos", align_bytes=64)
            dst = by_position[g][:].rearrange("p t (b m) j -> p b t m j", m=2)
            src = raw[g][:].rearrange("p j (b m t) -> p b t m j", m=2, t=SLOTS)
            cut = scalar_columns // 2
            nc.vector.tensor_copy(out=dst[:, cut:], in_=src[:, cut:])
            nc.scalar.copy(out=dst[:, 0:cut], in_=src[:, 0:cut])

        def quantize_by_position(g):
            by_position_mx[g] = quantize("ap%d" % g, by_position[g][:].rearrange("p t m j -> p (t m j)"), E4M3)

        def quantize_by_channel(g):
            by_channel_mx[g] = quantize("ac%d" % g, by_channel[g][:].rearrange("p s w -> p (s w)").bitcast(BF16), E4M3)

        def gram_pass(h, t, g):
            if g == 0:
                gram[h, t] = bank(SLOTS * h + t)
            codes, scales = by_position_mx[g]
            nc.tensor.matmul_mx(
                out=gram[h, t][:],
                lhsT=codes[:, t * P:(t + 1) * P].bitcast(E4M3), lhsT_scale=scales[:, t * P:(t + 1) * P],
                rhs=b_code[h, g].bitcast(E2M1), rhs_scale=b_scale[g // 4][:, g % 4, HALF * h:HALF * (h + 1)],
                start=(g == 0), stop=(g == GROUPS - 1))

        def gram_group(h, g):
            for t in range(SLOTS):
                gram_pass(h, t, g)

        def weigh_target(h, t):
            if t == 0:
                weighted[h] = keep.tile([P, SLOTS, HALF], F32, name="wtgt%d" % h)
            nc.scalar.activation(out=weighted[h][:, t, :], in_=tgt[h, t], func=COPY, scale=vectors[:, WEIGHT_ROW, t:t + 1])

        def error(h, t):
            if t == 0:
                err[h] = keep.tile([P, SLOTS, HALF], BF16, name="err%d" % h)
            nc.vector.scalar_tensor_tensor(
                out=err[h][:, t, :], in0=gram[h, t][:], scalar=vectors[:, WEIGHT_ROW, t:t + 1], in1=weighted[h][:, t, :],
                op0=ALU.mult, op1=ALU.subtract)

        def quantize_error(h, scalar_columns):
            grouped = keep.tile([P, HALF, SLOTS], BF16, name="eg%d" % h, align_bytes=64)
            dst = grouped[:].rearrange("p (c i) t -> p c t i", i=4)
            src = err[h][:].rearrange("p t (c i) -> p c t i", i=4)
            cut = scalar_columns // 4
            nc.vector.tensor_copy(out=dst[:, cut:], in_=src[:, cut:])
            if cut:
                nc.scalar.copy(out=dst[:, 0:cut], in_=src[:, 0:cut])
            err_mx[h] = quantize("e%d" % h, grouped[:].rearrange("p n t -> p (n t)"), E5M2)

        def out_tile(g, j, h, bk, on_vector):
            if j == 0 and h == 0:
                result[g] = outs.tile([P, SLOTS, COLUMNS], F32, name="result")
            acc = bank(bk)
            codes, scales = by_channel_mx[g]
            e_codes, e_scales = err_mx[h]
            nc.tensor.matmul_mx(
                out=acc[:],
                lhsT=codes[:, j * P:(j + 1) * P].bitcast(E4M3), lhsT_scale=scales[:, j * P:(j + 1) * P],
                rhs=e_codes[:].bitcast(E5M2), rhs_scale=e_scales[:], start=True, stop=True)
            dst = result[g][:, j, HALF * h:HALF * (h + 1)]
            if on_vector:
                nc.vector.tensor_scalar_mul(out=dst, in0=acc[:], scalar1=vectors[:, g, j:j + 1])
            else:
                nc.scalar.activation(out=dst, in_=acc[:], func=COPY, scale=vectors[:, g, j:j + 1])

        def store(g, js, cols):
            rows = out[g * PASS:(g + 1) * PASS, :].rearrange("(p j) n -> p j n", j=SLOTS)
            nc.sync.dma_start(out=rows[:, js, cols], in_=result[g][:, js, cols])

        def row_pair(g, j0):
            for j in (j0, j0 + 1):
                for h in range(2):
                    out_tile(g, j, h, (8 * g + 2 * j + h) % 6, on_vector=(h == 1))

        clear_scales(0)
        nc.vector.memset(vector_rows[:].bitcast(I32), 0)
        clear_scales(1)
        make_identity(nc, ident[:])

        load_a(0)
        load_scales(0)
        load_b([0], [0, 1])
        load_a(1)
        load_vectors()
        load_b([1], [0, 1])
        load_a(2)
        load_a(3)
        load_b([2, 3], [0, 1])
        load_a(4)
        load_scales(1)
        load_a(5)
        load_b([4, 5], [0])
        load_a(6)
        load_a(7)
        load_b([6, 7], [0])
        load_target(0)
        load_b([4, 5, 6, 7], [1])
        load_target(1)

        turn_a(0, (4, 5))
        interleave_a(0, SCALAR_A_FREE)
        quantize_by_position(0)
        copy_turned(0, 0, True)
        copy_turned(0, 1, False)
        gram_group(0, 0)
        turn_a(1, (6, 7))
        turn_vectors(4)
        interleave_a(1, SCALAR_A)
        quantize_by_channel(0)
        quantize_by_position(1)
        gram_group(0, 1)
        interleave_a(2, SCALAR_A)
        copy_vectors()
        copy_turned(1, 0, True)
        copy_turned(1, 1, False)
        quantize_by_position(2)
        gram_group(1, 0)
        gram_group(0, 2)

        interleave_a(3, SCALAR_A)
        quantize_by_position(3)
        gram_group(1, 1)
        gram_group(0, 3)
        interleave_a(4, SCALAR_A)
        quantize_by_channel(1)
        quantize_by_position(4)
        gram_group(1, 2)
        gram_group(0, 4)
        interleave_a(5, SCALAR_A_FREE)
        quantize_by_position(5)
        gram_group(0, 5)
        interleave_a(6, SCALAR_A_FREE)
        quantize_by_position(6)
        gram_pass(1, 0, 3)
        gram_pass(1, 1, 3)
        gram_group(0, 6)

        last = GROUPS - 1
        interleave_a(last, SCALAR_A_LAST)
        by_position_mx[last] = mx_tiles("ap%d" % last)
        for t in range(SLOTS):
            codes, scales = by_position_mx[last]
            nc.vector.quantize_mx(
                out=codes[:, t * P:(t + 1) * P].bitcast(E4M3), scales=scales[:, t * P:(t + 1) * P],
                in_=by_position[last][:, t, :, :].rearrange("p m j -> p (m j)"))
            gram_pass(0, t, last)
        for t in range(SLOTS):
            weigh_target(0, t)
            error(0, t)
        weigh_target(1, 0)
        weigh_target(1, 1)
        quantize_error(0, SCALAR_E)
        weigh_target(1, 2)
        weigh_target(1, 3)

        gram_pass(1, 2, 3)
        gram_pass(1, 3, 3)
        for t in range(SLOTS - 1):
            for g in range(4, GROUPS):
                gram_pass(1, t, g)
            error(1, t)
        gram_pass(1, 3, 4)

        for n in range(EARLY * SLOTS):
            g, j = divmod(n, SLOTS)
            out_tile(g, j, 0, j, on_vector=False)
            if n < 2:
                store(g, slice(j, j + 1), slice(0, HALF))
            elif j % 2 == 1:
                store(g, slice(j - 1, j + 1), slice(0, HALF))
            if 5 + n < GROUPS:
                gram_pass(1, 3, 5 + n)
            if 5 + n == last:
                error(1, 3)
                quantize_error(1, 0)
            if n == EARLY * SLOTS - 2:
                turn_a(EARLY, (4, 5))

        for n in range(EARLY * SLOTS):
            g, j = divmod(n, SLOTS)
            out_tile(g, j, 1, j, on_vector=(j % 2 == 1))
            if g == 0 and j % 2 == 1:
                store(g, slice(j - 1, j + 1), slice(HALF, COLUMNS))
            if g > 0 and j == SLOTS - 1:
                store(g, slice(0, SLOTS), slice(HALF, COLUMNS))
            if n < 2:
                copy_turned(EARLY, n, on_vector=(n == 0))
            if n == SLOTS:
                quantize_by_channel(EARLY)

        for g in range(EARLY, GROUPS):
            in_two = g < EARLY + 2
            if g < last:
                turn_a(g + 1, (6, 7))
                copy_turned(g + 1, 0, False)
                copy_turned(g + 1, 1, True)
            row_pair(g, 0)
            if in_two:
                store(g, slice(0, 2), slice(0, COLUMNS))
            if g < last:
                quantize_by_channel(g + 1)
            row_pair(g, 2)
            store(g, slice(2 if in_two else 0, SLOTS), slice(0, COLUMNS))
